import numpy as np
import ml_dtypes


def mxq(x, axis, fmt="e4m3"):
    dtype, down = {"e4m3": (ml_dtypes.float8_e4m3fn, 7), "e5m2": (ml_dtypes.float8_e5m2, 14)}[fmt]
    v = np.moveaxis(np.asarray(x, np.float32).astype(ml_dtypes.bfloat16).astype(np.float64), axis, -1)
    blocks = v.reshape(v.shape[:-1] + (-1, 32))
    amax = np.abs(blocks).max(-1, keepdims=True)
    byte = np.maximum(np.where(amax > 0, np.frexp(amax)[1] - 1 + 127, 0) - down, 1)
    scale = np.exp2(byte - 127.0)
    codes = (blocks / scale).astype(np.float32).astype(dtype).astype(np.float64)
    return np.moveaxis((codes * scale).reshape(v.shape), -1, axis)


WIDE = False


def mx_kscale(k):
    if not WIDE:
        return np.ones(k)
    levels = np.array([10, -10, 5, -5, 0])
    if k % 512:
        return np.exp2(np.random.permutation(np.resize(levels, k // 32))).repeat(32)
    a = np.empty((k // 512, 16))
    for p in range(k // 512):
        a[p, :8] = np.random.permutation(np.resize(levels, 8))
        for g in range(8):
            far = levels[np.abs(levels - a[p, g]) >= 10]
            a[p, g + 8] = far[np.random.randint(len(far))]
    return np.exp2(a.ravel()).repeat(32)


BF16 = ml_dtypes.bfloat16


def bf(x):
    return np.asarray(x, np.float32).astype(BF16)


def f64(x):
    return np.asarray(x).astype(np.float64)


E2M1 = np.array([0.0, 0.5, 1.0, 1.5, 2.0, 3.0, 4.0, 6.0, -0.0, -0.5, -1.0, -1.5, -2.0, -3.0, -4.0, -6.0])


def pack_weight(w, fmt):
    k, n = w.shape
    w = f64(bf(w)).reshape(k // 32, 32, n)
    amax = np.abs(w).max(1)
    if fmt == "e4m3":
        byte = np.frexp(amax)[1] - 1 + 127 - 7
    else:
        mant, ex = np.frexp(amax / 6.0)
        byte = np.where(mant > 0.5, ex, ex - 1) + 127
    byte = np.clip(np.where(amax > 0, byte, 1), 1, 254)
    scaled = (w * np.exp2(127.0 - byte)[:, None, :]).reshape(k, n).astype(np.float32)
    by_word = np.ascontiguousarray(scaled.reshape(k // 512, 128, 4, n).transpose(0, 1, 3, 2))
    if fmt == "e4m3":
        words = by_word.astype(ml_dtypes.float8_e4m3fn).view(np.uint8)
    else:
        c = by_word.astype(ml_dtypes.float4_e2m1fn).view(np.uint8) & 0xF
        words = c[..., 0::2] | (c[..., 1::2] << 4)
    return np.ascontiguousarray(words), np.ascontiguousarray(byte.astype(np.uint8).reshape(k // 512, 16, n))


def unpack_weight(words, scales, fmt):
    g, p, n, _ = words.shape
    if fmt == "e4m3":
        vals = np.ascontiguousarray(words).view(ml_dtypes.float8_e4m3fn).astype(np.float64)
    else:
        nib = np.empty((g, p, n, 4), np.uint8)
        nib[..., 0::2] = words & 0xF
        nib[..., 1::2] = words >> 4
        vals = E2M1[nib]
    vals = vals * np.repeat(np.exp2(scales.astype(np.float64) - 127.0), 8, axis=1)[..., None]
    return vals.transpose(0, 1, 3, 2).reshape(g * 512, n)
def pack4(w):
    words, scales = pack_weight(w, "e2m1")
    return words.reshape(words.shape[0], 128, -1), scales


def unpack4(words, scales):
    return unpack_weight(words.reshape(words.shape[0], 128, -1, 2), scales, "e2m1")


def planes(Y):
    n, m = Y.shape
    b = f64(bf(Y)).reshape(n // 32, 32, m)
    amax = np.abs(b).max(1)
    byte = np.clip(np.where(amax > 0, np.frexp(amax)[1] - 1 + 127 - 7, 1), 1, 254)
    codes = (b * np.exp2(127.0 - byte)[:, None, :]).reshape(n, m).astype(np.float32).astype(ml_dtypes.float8_e4m3fn).view(np.uint8)
    words = codes.reshape(n // 512, 128, 4, m).transpose(0, 1, 3, 2)
    return np.ascontiguousarray(words), np.ascontiguousarray(byte.astype(np.uint8).reshape(n // 512, 16, m))


U, I = 512, 1536

CORR = 0.33
P1, P2, P3 = 0.2, 0.3, 0.8
OFFSET = 0.3

def item_weights(size):
    return size * np.random.randn(I, I) / np.sqrt(I) * (1.0 - np.eye(I))

def setup_inputs():
    s = mx_kscale(I)
    z = np.random.randn(I)
    X = np.random.randn(U, I) * s[None, :]
    B1_words, B1_scales = pack4(item_weights(CORR) / s[:, None])
    B2 = item_weights(CORR) / s[:, None]
    B3 = item_weights(1.0) / s[:, None]
    d1 = np.exp(-P1 * z) * s
    d2 = np.exp(-P2 * z) * s
    d3 = np.exp(-P3 * z)
    b = OFFSET * z
    return {"X": bf(X), "B1_words": B1_words, "B1_scales": B1_scales, "B2": bf(B2), "B3": bf(B3),
            "d1": bf(d1), "d2": bf(d2), "d3": bf(d3), "b": bf(b)}

def reference(X, B1_words, B1_scales, B2, B3, d1, d2, d3, b):
    X, B2, B3 = f64(X), f64(B2), f64(B3)
    d1, d2, d3, b = f64(d1), f64(d2), f64(d3), f64(b)
    B1 = unpack4(B1_words, B1_scales)
    H1 = X + d1 * (mxq(X, 1, "e4m3") @ B1)
    H2 = H1 + d2 * (mxq(H1, 1, "e4m3") @ mxq(B2, 0, "e4m3"))
    y = ((mxq(H2, 1, "e4m3") @ mxq(B3, 0, "e4m3")) - b) * d3
    Y = y.T
    words, scales = planes(Y)
    return y, words, scales

from contextlib import ExitStack

import concourse.mybir as mybir
from concourse.masks import make_identity

F32 = mybir.dt.float32
BF16 = mybir.dt.bfloat16
I32 = mybir.dt.int32
U32 = mybir.dt.uint32
U8 = mybir.dt.uint8
FP8X4 = mybir.dt.float8_e4m3fn_x4
FP4X4 = mybir.dt.float4_e2m1fn_x4
MULT = mybir.AluOpType.mult
ADD = mybir.AluOpType.add
IDENTITY = mybir.ActivationFunctionType.Identity

USERS, ITEMS = 512, 1536
P = 128
PACK = 4
GROUP = P * PACK
GROUPS = ITEMS // GROUP
USER_BLOCKS = USERS // P
FLOPS = 3 * 2 * USERS * ITEMS * ITEMS
PARTS = (1, 1, 1)
WEIGHT_PIECES = 1

ORDER = """
dl_0:G X_3:D X_0:D X_2:D X_1:D dt_0:P xp_3:V xt_3:P xa_3:S xp_0:V xt_0:P xp_2:V xt_2:P xb_3:V xp_1:V xt_1:P
dc_0:S xq_3:V xb_2:V B1_1:D m1_1_3:P xb_0:S xa_2:S B2_0_2:D xa_0:S xq_2:V xb_1:V i2_0_2_0:S m1_1_2:P xa_1:V
xq_0:V m1_1_0:P ac_1_3:V xq_1:V ac_1_2:S qb2_0_2:V B2_2:D i2_2_1_0:V i2_2_0_0:S i2_2_2_0:V B1_0:D m1_1_1:P
ac_1_1:S m1_0_1:P m1_0_2:P ac_1_0:S B2_1_0:D B2_1_2:D i2_1_0_0:V ac_0_1:S m1_0_3:P m1_0_0:P qb2_2_1:V t1_1_0:P
ac_0_2:S qb2_2_0:V ac_0_3:S qb2_2_2:V ac_0_0:S qb2_1_0:V t1_0_0:P s1_1_0_0:V s1_1_0_3:V B1_2:D s1_0_0_1:V
m1_2_2:P B2_0_0:D i2_0_0_0:S s1_0_0_0:V m1_2_1:P s1_0_0_2:V s1_0_0_3:V m1_2_0:P qb2_0_0:V s1_1_0_1:V
s1_1_0_2:V ac_2_0:V B2_1_1:D i2_1_1_0:S ac_2_2:S c1_0_0_1:V i2_1_2_0:G qb2_1_2:V qb2_1_1:V c1_0_0_0:G q1_0_0:V
m1_2_3:P ac_2_3:S ac_2_1:S t1_2_0:P B2_0_1:D B3_2:D i3_2_0_0:S n2_0_0_3:P i2_0_1_0:S n2_0_0_1:P s1_2_0_2:V
s1_2_0_0:V n2_2_0_1:P n2_0_0_2:P s1_2_0_3:V s1_2_0_1:V c1_2_0_0:S c1_1_0_1:V c1_2_0_1:V B3_0:D c1_1_0_0:G
n2_0_0_0:P n2_2_0_2:P q1_1_0:V n2_0_1_2:P q1_2_0:V qb3_2_0:V i3_0_0_0:S m2_0_0_2:P qb2_0_1:V i3_2_1_0:S
s2_0_0_2:V n2_0_1_0:P m2_0_0_0:P s2_0_0_0:V n2_0_1_1:P m2_0_0_1:P s2_0_0_1:V B3_1:D n2_0_1_3:P m2_0_0_3:P
n2_1_0_3:P n2_1_1_3:P s2_0_0_3:V m2_1_0_3:P s2_1_0_3:V n2_1_0_1:P qb3_0_0:V i3_1_0_0:S n2_1_1_1:P m2_1_0_1:P
n2_1_0_0:P n2_1_1_0:P qb3_2_1:V n2_1_0_2:P s2_1_0_1:V n2_2_0_0:P n2_2_1_0:P i3_0_1_0:G m2_1_0_0:P s2_1_0_0:V
m2_2_0_0:P i3_1_1_0:S n2_1_1_2:P m2_1_0_2:P s2_2_0_0:V c2_0_0_1:G n2_2_1_2:P s2_1_0_2:V c2_1_0_0:S m2_2_0_2:P
s2_2_0_2:V n2_2_1_1:P m2_2_0_1:P s2_2_0_1:V n2_2_0_3:P n2_2_1_3:P c2_0_0_0:G q2_0_0:V m2_2_0_3:P n3_0_0_3:P
s2_2_0_3:V n3_0_0_2:P qb3_0_1:V qb3_1_0:V n3_0_0_0:P n3_1_0_2:P n3_1_0_3:P n3_1_0_0:P c2_1_0_1:S q2_1_0:V
n3_0_1_2:P qb3_1_1:V n3_0_1_3:P c2_2_0_0:S i3_1_2_0:V n3_0_0_1:P n3_0_1_1:P n3_1_1_3:P n3_0_1_0:P c2_2_0_1:S
i3_2_2_0:S n3_1_0_1:P n3_1_1_1:P n3_1_1_2:P q2_2_0:V m3_1_0_1:P s3_1_0_1:S m3_1_0_2:P s3_1_0_2:S i3_0_2_0:V
qb3_1_2:V m3_1_0_3:P n3_1_1_0:P m3_1_0_0:P m3_0_0_2:P qb3_0_2:V m3_0_0_3:P m3_0_0_0:P m3_0_0_1:P n3_2_0_0:P
s3_1_0_0:S s3_1_0_3:V n3_2_1_0:P n3_2_0_1:P s3_0_0_3:S qb3_2_2:V s3_0_0_2:V s3_0_0_1:V s3_0_0_0:S t3_1_1:P
oc_1_1:S st_1_1:D c3_1_0_0:G t3_1_3:P t3_1_0:P oc_1_3:S st_1_3:D t3_0_2:P oc_0_2:S c3_1_0_1:V oc_1_0:V
c3_0_0_1:S t3_0_1:P oc_0_1:V st_0_2:D t3_0_3:P oc_0_3:V m3_2_0_0:P n3_2_1_1:P st_1_0:D m3_2_0_1:P st_0_1:D
n3_2_0_3:P q3_1_0:V st_0_3:D n3_2_0_2:P n3_2_1_3:P m3_2_0_3:P n3_2_1_2:P c3_0_0_0:G q3_0_0:V m3_2_0_2:P
s3_2_0_2:V sq_1_0:D s3_2_0_1:S sq_0_0:D t3_1_2:P s3_2_0_0:S s3_2_0_3:S oc_1_2:S st_1_2:D t3_0_0:P oc_0_0:V
t3_2_2:P st_0_0:D oc_2_2:S st_2_2:D t3_2_3:P oc_2_3:S st_2_3:D t3_2_0:P c3_2_0_0:V c3_2_0_1:V oc_2_0:S
st_2_0:D q3_2_0:V sq_2_0:D t3_2_1:P sz_0:D oc_2_1:S st_2_1:D
"""


def tile_debiased_item_scores_k1_kernel(
    tc, X, B1_words, B1_scales, B2, B3, d1, d2, d3, b, out_0, out_1, out_2
):
    nc = tc.nc
    weights = {2: B2, 3: B3}

    with ExitStack() as ctx:
        keep = ctx.enter_context(tc.tile_pool(name="keep", bufs=1))
        psum = ctx.enter_context(tc.psum_pool(name="psum", bufs=1))
        ctx.enter_context(tc.manual_schedule())

        kinds = {
            "bank": (psum, [P, GROUP], F32, 8),
            "rows": (keep, [P, GROUP], F32, 8),
            "grouped": (keep, [P, GROUP * PACK], BF16, 5),
            "raw": (keep, [P, PACK, ITEMS], BF16, 5),
        }
        free = {kind: list(range(spec[3])) for kind, spec in kinds.items()}
        held = {}

        def take(kind, key, readers):
            if key not in held:
                pool, shape, dtype, count = kinds[kind]
                slot = free[kind].pop(0)
                name = "%s%d" % (kind, slot)
                if kind == "bank":
                    buffer = pool.tile(shape, dtype, name=name, tag=name)
                else:
                    buffer = pool.tile(shape, dtype, name=name, tag=name, align_bytes=64)
                held[key] = [buffer, kind, slot, readers]
            return held[key][0]

        def read(key):
            entry = held[key]
            entry[3] -= 1
            if entry[3] == 0:
                free[entry[1]].append(entry[2])
            return entry[0]

        def copy(engine, out, in_):
            if engine == "V":
                nc.vector.tensor_copy(out=out, in_=in_)
            elif engine == "S":
                nc.scalar.copy(out=out, in_=in_)
            else:
                nc.gpsimd.tensor_scalar(out=out, in0=in_, scalar1=1.0, scalar2=0.0, op0=MULT, op1=ADD)

        identity = keep.tile([P, P], F32, align_bytes=64)
        x_rows = keep.tile([P, USER_BLOCKS, ITEMS], BF16, name="x_rows", tag="x_rows", align_bytes=64)
        x_grouped = keep.tile([P, GROUPS, USERS * PACK], BF16, align_bytes=64)
        b1_words = [keep.tile([P, GROUPS, 2 * GROUP], U8, name="b1_words%d" % c, align_bytes=64) for c in range(GROUPS)]
        b1_scales = keep.tile([P, GROUPS, ITEMS], U8, align_bytes=64)
        w_codes = {s: keep.tile([P, GROUPS, ITEMS], U32, name="w_codes%d" % s, align_bytes=64) for s in (2, 3)}
        w_scales = {s: keep.tile([P, GROUPS, ITEMS], U8, name="w_scales%d" % s, align_bytes=64) for s in (2, 3)}
        planes = {}

        def plane(s):
            if s not in planes:
                slot = 0 if s == 2 else s
                planes[s] = (
                    keep.tile([P, GROUPS, USERS], U32, name="codes%d" % s, tag="codes%d" % slot, align_bytes=64),
                    keep.tile([P, GROUPS, USERS], U8, name="scales%d" % s, tag="scales%d" % slot, align_bytes=64),
                )
            return planes[s]

        h1 = [keep.tile([P, PACK, USERS], F32, name="wide%d" % c, tag="wide%d" % c, align_bytes=64) for c in range(GROUPS)]
        late = {}

        def h2_tile():
            if "h2" not in late:
                late["h2"] = keep.tile([P, GROUPS, PACK, USERS], BF16, name="h2", tag="x_rows", align_bytes=64)
            return late["h2"]

        def y_tile(c):
            if c not in late:
                late[c] = keep.tile([P, PACK, USERS], F32, name="y%d" % c, tag="wide%d" % c, align_bytes=64)
            return late[c]

        vec_rows = keep.tile([P, ITEMS], BF16, align_bytes=64)
        vec = keep.tile([P, GROUPS, 4, PACK], F32, align_bytes=64)
        offset = keep.tile([P, GROUPS, PACK], F32, align_bytes=64)

        nc.vector.memset(vec_rows[:].bitcast(I32), 0)
        nc.vector.memset(b1_scales[:].bitcast(I32), 0)
        make_identity(nc, identity[:])

        def turn(words, name, sorted_words):
            for g in range(GROUPS):
                bank = take("bank", (name, g // 2), 1)
                for half in range(2):
                    nc.tensor.transpose(
                        bank[:, block((g % 2) * 2 + half, P)],
                        words[:, block(2 * g + half, P)] if sorted_words else words[:, 256 * g + half : 256 * (g + 1) : 2],
                        identity[:],
                    )

        def block(i, width):
            return slice(i * width, (i + 1) * width)

        def pieces(stage):
            return max(1, 2 // PARTS[stage - 1])

        def multiply(stage, c, h, t, g, bank):
            width = USERS // PARTS[stage - 1]
            users = block(h, width)
            cols = block(c * PACK + t, P)
            nc.tensor.matmul_mx(
                out=bank[:, block(t % PARTS[stage - 1], width)],
                lhsT=w_codes[stage][:, g, cols].bitcast(FP8X4),
                lhsT_scale=w_scales[stage][:, g, cols],
                rhs=plane(stage - 1)[0][:, g, users].bitcast(FP8X4),
                rhs_scale=plane(stage - 1)[1][:, g, users],
                start=(g == 0),
                stop=(g == GROUPS - 1),
            )


        for token in ORDER.split():
            step, engine = token.split(":")
            fields = step.split("_")
            kind = fields[0]
            at = [int(f) for f in fields[1:]]
            if kind == "dl":
                for i, vector in enumerate((d1, d2, d3, b)):
                    nc.scalar.dma_start(out=vec_rows[i : i + 1, :], in_=vector.rearrange("(o n) -> o n", o=1))
                for q in range(4):
                    nc.gpsimd.dma_start(
                        out=b1_scales[32 * q : 32 * q + 4, :, :].bitcast(I32),
                        in_=B1_scales[:, 4 * q : 4 * q + 4, :].rearrange("g r n -> r g n").bitcast(I32),
                    )
            elif kind == "X":
                nc.sync.dma_start(out=x_rows[:, at[0], :], in_=X[block(at[0], P), :])
            elif kind == "B1":
                nc.sync.dma_start(
                    out=b1_words[at[0]][:].bitcast(I32),
                    in_=B1_words.rearrange("g p n -> p g n")[:, :, block(at[0], 2 * GROUP)].bitcast(I32),
                )
            elif kind in ("B2", "B3"):
                stage = int(kind[1])
                g = at[0]
                cols = block(at[1], GROUP) if len(at) == 2 else slice(0, ITEMS)
                raw = take("raw", ("raw", stage, g), GROUPS * WEIGHT_PIECES)
                nc.sync.dma_start(
                    out=raw[:, :, cols],
                    in_=weights[stage][block(g, GROUP), cols].rearrange("(p j) n -> p j n", j=PACK),
                )
            elif kind == "xt":
                turn(read(("xp", at[0]))[:].bitcast(F32), "xt%d" % at[0], True)
            elif kind == "xp":
                words = take("grouped", ("xp", at[0]), 1)[:].bitcast(F32)[:, : ITEMS // 2]
                copy(
                    engine,
                    words.rearrange("p (g h m) -> p g h m", g=GROUPS, h=2),
                    x_rows[:, at[0], :].bitcast(F32).rearrange("p (g m h) -> p g h m", g=GROUPS, h=2),
                )
            elif kind == "dt":
                turn(vec_rows[:].bitcast(F32), "dt", False)
            elif kind == "dc":
                banks = [read(("dt", 0)), read(("dt", 1))]
                for g in range(GROUPS):
                    pairs = banks[g // 2][:, block(g % 2, 2 * P)].bitcast(BF16)
                    nc.scalar.activation(
                        out=vec[:, g].rearrange("p i (h e) -> p i h e", e=2),
                        in_=pairs.rearrange("p (h u e) -> p u h e", h=2, e=2)[:, 0:4],
                        func=IDENTITY,
                    )
                nc.gpsimd.tensor_tensor(out=offset[:], in0=vec[:, :, 3, :], in1=vec[:, :, 2, :], op=MULT)
                nc.gpsimd.tensor_scalar(out=offset[:], in0=offset[:], scalar1=-1.0, scalar2=0.0, op0=MULT, op1=ADD)
            elif kind in ("xa", "xb"):
                ub = at[0]
                first, count = (0, 2) if kind == "xa" else (2, 1)
                bank = read(("xt%d" % ub, first // 2))
                words = x_grouped[:].bitcast(F32).rearrange("p g (u h) -> p g u h", h=2)
                copy(
                    engine,
                    words[:, first : first + count, block(ub, P), :],
                    bank[:, : count * 2 * P].rearrange("p (g h u) -> p g u h", h=2, u=P),
                )
            elif kind == "xq":
                ub = at[0]
                for g in range(GROUPS):
                    nc.vector.quantize_mx(
                        out=plane(0)[0][:, g, block(ub, P)].bitcast(FP8X4),
                        scales=plane(0)[1][:, g, block(ub, P)],
                        in_=x_grouped[:, g, block(ub, P * PACK)],
                    )
            elif kind == "m1":
                c, ub = at
                bank = take("bank", ("m1", c, ub), 1)
                for g in range(GROUPS):
                    nc.tensor.matmul_mx(
                        out=bank[:],
                        lhsT=plane(0)[0][:, g, block(ub, P)].bitcast(FP8X4),
                        lhsT_scale=plane(0)[1][:, g, block(ub, P)],
                        rhs=b1_words[c][:, g, :].bitcast(FP4X4),
                        rhs_scale=b1_scales[:, g, block(c, GROUP)],
                        start=(g == 0),
                        stop=(g == GROUPS - 1),
                    )
            elif kind == "ac":
                c, ub = at
                rows = take("rows", ("ac", c, ub), 1)
                bank = read(("m1", c, ub))
                copy(
                    engine,
                    rows[:].rearrange("p (t m) -> p t m", t=PACK),
                    bank[:].rearrange("p (m t) -> p t m", t=PACK),
                )
            elif kind == "t1":
                c, h = at
                parts = PARTS[0]
                blocks = USER_BLOCKS // parts
                banks = [take("bank", (1, c, h, i), parts) for i in range(PACK // parts)]
                for i in range(blocks):
                    rows = read(("ac", c, h * blocks + i))
                    for t in range(PACK):
                        nc.tensor.transpose(
                            banks[t // parts][:, block((t % parts) * blocks + i, P)],
                            rows[:, block(t, P)],
                            identity[:],
                        )
            elif kind in ("i2", "i3"):
                stage = int(kind[1])
                g, c, half = at
                grouped = take("grouped", ("w", stage, g, c), 1)
                raw = read(("raw", stage, g))[:, :, block(c, GROUP)]
                copy(
                    engine,
                    grouped[:].rearrange("p (t m j) -> p m j t", t=PACK, j=PACK)[:, block(half, P // WEIGHT_PIECES)],
                    raw.rearrange("p j (m t) -> p m j t", t=PACK)[:, block(half, P // WEIGHT_PIECES)],
                )
            elif kind in ("qb2", "qb3"):
                stage = int(kind[2])
                g, c = at
                grouped = read(("w", stage, g, c))
                nc.vector.quantize_mx(
                    out=w_codes[stage][:, g, block(c, GROUP)].bitcast(FP8X4),
                    scales=w_scales[stage][:, g, block(c, GROUP)],
                    in_=grouped[:],
                )
            elif kind in ("n2", "n3"):
                stage = int(kind[1])
                c, g, t = at
                multiply(stage, c, 0, t, g, take("bank", (stage, c, 0, t), 1))
            elif kind in ("m2", "m3"):
                stage = int(kind[1])
                c, h, pair = at
                parts = PARTS[stage - 1]
                bank = take("bank", (stage, c, h, pair), parts)
                if parts == 1:
                    multiply(stage, c, 0, pair, GROUPS - 1, bank)
                else:
                    for t in range(pair * parts, (pair + 1) * parts):
                        for g in range(GROUPS):
                            multiply(stage, c, h, t, g, bank)
            elif kind in ("s1", "s2", "s3"):
                stage = int(kind[1])
                c, h, t = at
                parts = PARTS[stage - 1]
                width = USERS // parts
                users = block(h, width)
                sums = read((stage, c, h, t // parts))[:, block(t % parts, width)]
                gain = vec[:, c, stage - 1, t : t + 1]
                if stage == 1:
                    x_items = x_grouped[:, c, :].rearrange("p (u t) -> p t u", t=PACK)
                    nc.vector.scalar_tensor_tensor(
                        out=h1[c][:, t, users], in0=sums, scalar=gain, in1=x_items[:, t, users], op0=MULT, op1=ADD
                    )
                elif stage == 2:
                    nc.vector.scalar_tensor_tensor(
                        out=h2_tile()[:, c, t, users], in0=sums, scalar=gain, in1=h1[c][:, t, users], op0=MULT, op1=ADD
                    )
                elif engine == "S":
                    nc.scalar.activation(
                        out=y_tile(c)[:, t, users], in_=sums, func=IDENTITY, scale=gain, bias=offset[:, c, t : t + 1]
                    )
                else:
                    nc.vector.tensor_scalar(
                        out=y_tile(c)[:, t, users], in0=sums, scalar1=gain, scalar2=offset[:, c, t : t + 1],
                        op0=MULT, op1=ADD,
                    )
            elif kind in ("c1", "c2", "c3"):
                stage = int(kind[1])
                c, h, piece = at
                width = USERS // PARTS[stage - 1] // pieces(stage)
                source = h1[c][:] if stage == 1 else (h2_tile()[:, c] if stage == 2 else y_tile(c)[:])
                grouped = take("grouped", ("h", stage, c, h), 1)
                run = 1 if engine == "G" else 4
                copy(
                    engine,
                    grouped[:, block(piece, width * PACK)].rearrange("p (u i t) -> p u t i", i=run, t=PACK),
                    source[:, :, block(h * pieces(stage) + piece, width)].rearrange("p t (u i) -> p u t i", i=run),
                )
            elif kind in ("q1", "q2", "q3"):
                stage = int(kind[1])
                c, h = at
                width = USERS // PARTS[stage - 1]
                grouped = read(("h", stage, c, h))
                nc.vector.quantize_mx(
                    out=plane(stage)[0][:, c, block(h, width)].bitcast(FP8X4),
                    scales=plane(stage)[1][:, c, block(h, width)],
                    in_=grouped[:, : width * PACK],
                )
            elif kind == "t3":
                c, ub = at
                bank = take("bank", ("t3", c, ub), 1)
                for t in range(PACK):
                    nc.tensor.transpose(bank[:, block(t, P)], y_tile(c)[:, t, block(ub, P)], identity[:])
            elif kind == "oc":
                c, ub = at
                rows = take("rows", ("oc", c, ub), 1)
                bank = read(("t3", c, ub))
                copy(
                    engine,
                    rows[:].rearrange("p (m t) -> p m t", t=PACK),
                    bank[:].rearrange("p (t m) -> p m t", t=PACK),
                )
            elif kind == "st":
                c, ub = at
                nc.sync.dma_start(out=out_0[block(ub, P), block(c, GROUP)], in_=read(("oc", c, ub))[:])
            elif kind == "sq":
                c, h = at
                users = block(h, USERS // PARTS[2])
                nc.sync.dma_start(
                    out=out_1[c].rearrange("p m t -> p (m t)").bitcast(I32)[:, users],
                    in_=plane(3)[0][:, c, users].bitcast(I32),
                )
            else:
                for q in range(4):
                    nc.sync.dma_start(
                        out=out_2[:, 4 * q : 4 * q + 4, :].rearrange("g r m -> r g m").bitcast(I32),
                        in_=plane(3)[1][32 * q : 32 * q + 4, :, :].bitcast(I32),
                    )
